import numpy as np
import ml_dtypes


def mxq(x, axis, fmt="e4m3"):
    dtype, down = {"e4m3": (ml_dtypes.float8_e4m3fn, 7), "e5m2": (ml_dtypes.float8_e5m2, 14)}[fmt]
    v = np.moveaxis(np.asarray(x, np.float32).astype(ml_dtypes.bfloat16).astype(np.float64), axis, -1)
    blocks = v.reshape(v.shape[:-1] + (-1, 32))
    amax = np.abs(blocks).max(-1, keepdims=True)
    byte = np.maximum(np.where(amax > 0, np.frexp(amax)[1] - 1 + 127, 0) - down, 1)
    scale = np.exp2(byte - 127.0)
    codes = (blocks / scale).astype(np.float32).astype(dtype).astype(np.float64)
    return np.moveaxis((codes * scale).reshape(v.shape), -1, axis)


WIDE = False


def mx_kscale(k):
    if not WIDE:
        return np.ones(k)
    levels = np.array([10, -10, 5, -5, 0])
    if k % 512:
        return np.exp2(np.random.permutation(np.resize(levels, k // 32))).repeat(32)
    a = np.empty((k // 512, 16))
    for p in range(k // 512):
        a[p, :8] = np.random.permutation(np.resize(levels, 8))
        for g in range(8):
            far = levels[np.abs(levels - a[p, g]) >= 10]
            a[p, g + 8] = far[np.random.randint(len(far))]
    return np.exp2(a.ravel()).repeat(32)


def f64(x):
    return np.asarray(x).astype(np.float64)


def striped(idx):
    return np.tile(idx.reshape(-1, 16).T, (8, 1)).astype(np.uint16)


def unstriped(offs):
    return offs[:16].T.reshape(-1).astype(np.int64)


def relu2(v):
    return np.maximum(v, 0.0) ** 2


K, T, E, C, N = 1024, 768, 18, 128, 128
TOP = 3


def by_expert(wq, xq):
    return np.concatenate([wq[e].T @ xq[:, e * C:(e + 1) * C] for e in range(E)], axis=1)


def setup_inputs():
    n = np.random.standard_normal
    s = mx_kscale(K)[:, None]
    deal = np.repeat(np.arange(E), C).reshape(TOP, T)[:, np.random.permutation(T)]
    deal = np.take_along_axis(deal, np.argsort(np.random.rand(TOP, T), axis=0), axis=0)
    for _ in range(8):
        s_, t_ = np.random.permutation(T).reshape(2, -1); r = np.random.randint(TOP, size=T // 2); x, y = deal[r, s_].copy(), deal[r, t_].copy()
        ok = ~((deal[:, s_] == y).any(0) | (deal[:, t_] == x).any(0)); deal[r[ok], s_[ok]] = y[ok]; deal[r[ok], t_[ok]] = x[ok]
    order = np.lexsort((np.random.rand(TOP * T), deal.reshape(-1)))
    slot_token = order % T; pos = np.empty(TOP * T, np.int64); pos[order] = np.arange(TOP * T); pos = pos.reshape(TOP, T)
    g = np.random.uniform(0.5, 1.5, (TOP, T)); g = g / g.sum(0)
    return {
        "xT": (n((K, T)) * s).astype(np.float32),
        "w": (n((E + 1, K, N)) / np.sqrt(K) / s[None]).astype(np.float32),
        "b": (0.3 * n((N, E + 1))).astype(np.float32),
        "gate": np.stack([np.tile(r, (N, 1)) for r in g]).astype(np.float32),
        "offs": striped(slot_token),
        "pos1": striped(pos[0]),
        "pos2": striped(pos[1]),
        "pos3": striped(pos[2]),
    }


def reference(xT, w, b, gate, offs, pos1, pos2, pos3):
    idx = unstriped(offs)
    wq = mxq(f64(w), 1, "e4m3")
    xs = mxq(f64(xT), 0, "e4m3")
    ys = relu2((wq[E].T @ xs) + f64(b)[:, E:])
    xq = mxq(f64(xT)[:, idx], 0, "e4m3")
    y = by_expert(wq, xq)
    y = relu2(y + np.repeat(f64(b)[:, :E], C, axis=1))
    return ys + sum(f64(gate[r]) * y[:, unstriped(p)] for r, p in enumerate((pos1, pos2, pos3)))

@@ -1,0 +1,181 @@
+from contextlib import ExitStack
+
+import concourse.mybir as mybir
+
+K, T, E, C, N = 1024, 768, 18, 128, 128
+TOP = 3
+S = E * C
+FLOPS = 2 * K * N * (S + T)
+
+F32 = mybir.dt.float32
+BF16 = mybir.dt.bfloat16
+U32 = mybir.dt.uint32
+I32 = mybir.dt.int32
+U16 = mybir.dt.uint16
+U8 = mybir.dt.uint8
+FP8X4 = mybir.dt.float8_e4m3fn_x4
+ACT = mybir.ActivationFunctionType
+ALU = mybir.AluOpType
+
+P = 128
+PASSES = 2
+CHUNK = 512
+CHUNKS = [(s0, min(CHUNK, S - s0)) for s0 in range(0, S, CHUNK)]
+GROUP = 256
+HALF = T // 2
+VECTOR_PAIRS = (8,)
+
+
+def tile_moe_shr_lin_relu2_kernel(tc, xT, w, b, gate, offs, pos1, pos2, pos3, out):
+    nc = tc.nc
+    with ExitStack() as ctx:
+        keep = ctx.enter_context(tc.tile_pool(name="keep", bufs=1))
+        ring = ctx.enter_context(tc.tile_pool(name="ring", bufs=1))
+        psum = ctx.enter_context(tc.psum_pool(name="psum", bufs=1))
+
+        slot_list = keep.tile([P, S // 16], U16, name="slot_list")
+        x_rows = xT.rearrange("(g p h e) t -> g p h e t", g=PASSES, p=P, h=2)
+        x_head = [keep.tile([P, 2, HALF], F32, name="x_head%d" % q) for q in range(2)]
+        for q in range(2):
+            nc.sync.dma_start(x_head[q][:], x_rows[0, :, 0, :, q * HALF:(q + 1) * HALF])
+        nc.sync.dma_start(slot_list[:], offs)
+        x_next = keep.tile([P, 2, T], F32, name="x_next")
+        nc.sync.dma_start(x_next[:], x_rows[0, :, 1, :, :])
+        x_second = keep.tile([P, 2, 2, T], F32, name="x_second")
+        nc.sync.dma_start(x_second[:], x_rows[1])
+
+        pairs = [(e0, min(2, E + 1 - e0)) for e0 in range(0, E + 1, 2)]
+        bias = keep.tile([P, E + 1], F32, name="bias")
+        back_lists = [keep.tile([P, T // 16], U16, name="back_list%d" % r) for r in range(TOP)]
+        w_raw = []
+        for i, (e0, ne) in enumerate(pairs):
+            raw = ring.tile([P, ne * PASSES, 4, N], F32, name="w_raw%d" % i, tag="w_raw", bufs=5)
+            nc.sync.dma_start(raw[:], w[e0:e0 + ne].rearrange("e (g p j) n -> p (e g) j n", g=PASSES, p=P))
+            w_raw.append(raw)
+            if i == 1:
+                nc.sync.dma_start(bias[:], b)
+            if i == 4:
+                for lst, src in zip(back_lists, (pos1, pos2, pos3)):
+                    nc.sync.dma_start(lst[:], src)
+        gates = keep.tile([P, TOP, T], F32, name="gates")
+        nc.sync.dma_start(gates[:], gate.rearrange("r p t -> p r t"))
+
+        planes = keep.tile([P, 4 * T], U32, name="planes")
+
+        def plane(u):
+            return planes[:, u * T:(u + 1) * T]
+
+        for q in range(2):
+            nc.vector.tensor_copy(planes[:, q * HALF:(q + 1) * HALF].bitcast(BF16).rearrange("p (t e) -> p t e", e=2), x_head[q][:].rearrange("p e t -> p t e"))
+        nc.scalar.copy(plane(1).bitcast(BF16).rearrange("p (t e) -> p t e", e=2), x_next[:].rearrange("p e t -> p t e"))
+        nc.scalar.copy(planes[:, 2 * T:].bitcast(BF16).rearrange("p (h t e) -> p h t e", h=2, e=2), x_second[:].rearrange("p h e t -> p h t e"))
+
+        gathered = {}
+        x_codes = {}
+        x_scales = {}
+        w_codes = {}
+        w_scales = {}
+        y = keep.tile([P, S], F32, name="y")
+
+        def gather(c, g, h):
+            s0, n = CHUNKS[c]
+            if h == 0:
+                gathered[c, g] = ring.tile([P, 2 * n], U32, name="gathered%d_%d" % (c, g), tag="gathered", bufs=5)
+            nc.vector.tensor_copy(gathered[c, g][:, h * n:(h + 1) * n], plane(2 * g + h).indirect(slot_list[:, s0 // 16:(s0 + n) // 16]))
+
+        def quantise(woven, words, name):
+            codes = keep.tile([P, words], U32, name=name + "_codes", align_bytes=64)
+            scales = keep.tile([P, words], U8, name=name + "_scales", align_bytes=64)
+            nc.vector.quantize_mx(out=codes[:].bitcast(FP8X4), scales=scales[:], in_=woven)
+            return codes, scales
+
+        def weave_and_quantise(c, g, on_vector):
+            n = CHUNKS[c][1]
+            woven = ring.tile([P, 2 * n], U32, name="woven%d_%d" % (c, g), tag="woven", bufs=3, align_bytes=64)
+            if on_vector:
+                nc.vector.tensor_copy(woven[:].bitcast(I32).rearrange("p (s h) -> p s h", h=2), gathered[c, g][:].bitcast(I32).rearrange("p (h s) -> p s h", h=2))
+            else:
+                nc.scalar.copy(woven[:].rearrange("p (s h) -> p s h", h=2), gathered[c, g][:].rearrange("p (h s) -> p s h", h=2))
+            x_codes[c, g], x_scales[c, g] = quantise(woven[:].bitcast(BF16), n, "x%d_%d" % (c, g))
+
+        def weights(i):
+            e0, ne = pairs[i]
+            rounded = ring.tile([P, ne * PASSES * N * 4], BF16, name="w_bf%d" % i, tag="w_bf", bufs=3, align_bytes=64)
+            dst = rounded[:].rearrange("p (a c i j) -> p a c j i", a=ne * PASSES, i=4, j=4)
+            src = w_raw[i][:].rearrange("p a j (c i) -> p a c j i", i=4)
+            if i in VECTOR_PAIRS:
+                nc.vector.tensor_copy(dst, src)
+            else:
+                nc.scalar.copy(dst, src)
+            codes, scales = quantise(rounded[:], ne * PASSES * N, "w%d" % i)
+            for a in range(ne * PASSES):
+                w_codes[e0 + a // PASSES, a % PASSES] = codes[:, a * N:(a + 1) * N]
+                w_scales[e0 + a // PASSES, a % PASSES] = scales[:, a * N:(a + 1) * N]
+
+        def product(acc, e, codes, scales):
+            for g in range(PASSES):
+                nc.tensor.matmul_mx(out=acc, lhsT=w_codes[e, g].bitcast(FP8X4), lhsT_scale=w_scales[e, g],
+                                    rhs=codes[g].bitcast(FP8X4), rhs_scale=scales[g], start=(g == 0), stop=(g == PASSES - 1))
+
+        def experts(c):
+            s0, n = CHUNKS[c]
+            acc = psum.tile([P, n], F32, name="acc%d" % c, tag="acc", bufs=4)
+            positive = ring.tile([P, n], F32, name="positive%d" % c, tag="positive", bufs=2)
+            for q in range(n // C):
+                cols = slice(q * C, (q + 1) * C)
+                product(acc[:, cols], s0 // C + q, [x_codes[c, g][:, cols] for g in range(PASSES)], [x_scales[c, g][:, cols] for g in range(PASSES)])
+            for q in range(n // C):
+                cols = slice(q * C, (q + 1) * C)
+                e = s0 // C + q
+                nc.scalar.activation(positive[:, cols], acc[:, cols], ACT.Relu, bias=bias[:, e:e + 1])
+            nc.scalar.activation(y[:, s0:s0 + n], positive[:], ACT.Square)
+
+        last = len(CHUNKS) - 1
+        for h in range(2):
+            for c in range(len(CHUNKS)):
+                gather(c, 0, h)
+        early = {1: 0, 3: 1, 4: 2}
+        for c in range(len(CHUNKS)):
+            weave_and_quantise(c, 0, False)
+            gather(c, 1, 0)
+            gather(c, 1, 1)
+            if c in early:
+                weights(early[c])
+        weights(3)
+        later = {0: (4,), 1: (5, 6), 2: (7, 8), 3: (9,), 4: ()}
+        for c in range(len(CHUNKS)):
+            weave_and_quantise(c, 1, c == last)
+            if c > 0:
+                experts(c - 1)
+            for i in later[c]:
+                weights(i)
+        experts(last)
+
+        shared = keep.tile([P, T], F32, name="shared")
+        shared_acc = [psum.tile([P, 2 * GROUP], F32, name="shared_acc0"), psum.tile([P, GROUP], F32, name="shared_acc1")]
+        shared_positive = keep.tile([P, T], F32, name="shared_positive")
+        for q in range(T // GROUP):
+            woven = ring.tile([P, PASSES * 2 * GROUP], U32, name="woven_shared%d" % q, tag="woven", bufs=3, align_bytes=64)
+            nc.vector.tensor_copy(woven[:].bitcast(I32).rearrange("p (g t h) -> p g t h", g=PASSES, h=2),
+                                  planes[:].bitcast(I32).rearrange("p (g h t) -> p g t h", g=PASSES, h=2)[:, :, q * GROUP:(q + 1) * GROUP, :])
+            codes, scales = quantise(woven[:].bitcast(BF16), PASSES * GROUP, "xs%d" % q)
+            product(shared_acc[q // 2][:, (q % 2) * GROUP:(q % 2 + 1) * GROUP], E,
+                    [codes[:, g * GROUP:(g + 1) * GROUP] for g in range(PASSES)], [scales[:, g * GROUP:(g + 1) * GROUP] for g in range(PASSES)])
+        for acc, t0, n in ((shared_acc[0], 0, 2 * GROUP), (shared_acc[1], 2 * GROUP, GROUP)):
+            nc.scalar.activation(shared_positive[:, t0:t0 + n], acc[:], ACT.Relu, bias=bias[:, E:E + 1])
+            nc.scalar.activation(shared[:, t0:t0 + n], shared_positive[:, t0:t0 + n], ACT.Square)
+
+        for half in range(2):
+            toks = slice(half * HALF, (half + 1) * HALF)
+            terms = []
+            for r in range(TOP):
+                term = ring.tile([P, HALF], F32, name="term%d_%d" % (half, r), tag="term", bufs=6)
+                nc.vector.tensor_tensor(term[:], y[:].indirect(back_lists[r][:, half * HALF // 16:(half + 1) * HALF // 16]), gates[:, r, toks], ALU.mult)
+                terms.append(term)
+            first = ring.tile([P, HALF], F32, name="first%d" % half, tag="first", bufs=2)
+            second = ring.tile([P, HALF], F32, name="second%d" % half, tag="second", bufs=2)
+            total = ring.tile([P, HALF], F32, name="total%d" % half, tag="total", bufs=2)
+            nc.vector.tensor_tensor(first[:], terms[0][:], shared[:, toks], ALU.add)
+            nc.vector.tensor_tensor(second[:], terms[1][:], terms[2][:], ALU.add)
+            nc.vector.tensor_tensor(total[:], first[:], second[:], ALU.add)
+            nc.sync.dma_start(out[:, toks], total[:])

@@ -23,7 +23,8 @@ CHUNK = 512
 CHUNKS = [(s0, min(CHUNK, S - s0)) for s0 in range(0, S, CHUNK)]
 GROUP = 256
 HALF = T // 2
-VECTOR_PAIRS = (8,)
+GPSIMD_PAIRS = (1, 3, 5)
+VECTOR_PAIRS = ()
 
 
 def tile_moe_shr_lin_relu2_kernel(tc, xT, w, b, gate, offs, pos1, pos2, pos3, out):
@@ -33,81 +34,107 @@ def tile_moe_shr_lin_relu2_kernel(tc, xT, w, b, gate, offs, pos1, pos2, pos3, ou
         ring = ctx.enter_context(tc.tile_pool(name="ring", bufs=1))
         psum = ctx.enter_context(tc.psum_pool(name="psum", bufs=1))
 
+        pairs = [(e0, min(2, E + 1 - e0)) for e0 in range(0, E + 1, 2)]
+        w_raw = []
+
+        def load_weights(i):
+            e0, ne = pairs[i]
+            raw = ring.tile([P, ne * PASSES, 4, N], F32, name="w_raw%d" % i, tag="w_raw", bufs=5)
+            nc.sync.dma_start(raw[:], w[e0:e0 + ne].rearrange("e (g p j) n -> p (e g) j n", g=PASSES, p=P))
+            w_raw.append(raw)
+
         slot_list = keep.tile([P, S // 16], U16, name="slot_list")
         x_rows = xT.rearrange("(g p h e) t -> g p h e t", g=PASSES, p=P, h=2)
         x_head = [keep.tile([P, 2, HALF], F32, name="x_head%d" % q) for q in range(2)]
         for q in range(2):
             nc.sync.dma_start(x_head[q][:], x_rows[0, :, 0, :, q * HALF:(q + 1) * HALF])
         nc.sync.dma_start(slot_list[:], offs)
-        x_next = keep.tile([P, 2, T], F32, name="x_next")
-        nc.sync.dma_start(x_next[:], x_rows[0, :, 1, :, :])
-        x_second = keep.tile([P, 2, 2, T], F32, name="x_second")
-        nc.sync.dma_start(x_second[:], x_rows[1])
+        x_raw = {}
+        for u in range(1, 4):
+            x_raw[u] = keep.tile([P, 2, T], F32, name="x_raw%d" % u)
+            nc.sync.dma_start(x_raw[u][:], x_rows[u // 2, :, u % 2, :, :])
+            if u == 1:
+                load_weights(0)
 
-        pairs = [(e0, min(2, E + 1 - e0)) for e0 in range(0, E + 1, 2)]
         bias = keep.tile([P, E + 1], F32, name="bias")
         back_lists = [keep.tile([P, T // 16], U16, name="back_list%d" % r) for r in range(TOP)]
-        w_raw = []
-        for i, (e0, ne) in enumerate(pairs):
-            raw = ring.tile([P, ne * PASSES, 4, N], F32, name="w_raw%d" % i, tag="w_raw", bufs=5)
-            nc.sync.dma_start(raw[:], w[e0:e0 + ne].rearrange("e (g p j) n -> p (e g) j n", g=PASSES, p=P))
-            w_raw.append(raw)
-            if i == 1:
-                nc.sync.dma_start(bias[:], b)
+        for i in range(1, len(pairs)):
+            load_weights(i)
             if i == 4:
+                nc.sync.dma_start(bias[:], b)
                 for lst, src in zip(back_lists, (pos1, pos2, pos3)):
                     nc.sync.dma_start(lst[:], src)
         gates = keep.tile([P, TOP, T], F32, name="gates")
         nc.sync.dma_start(gates[:], gate.rearrange("r p t -> p r t"))
 
-        planes = keep.tile([P, 4 * T], U32, name="planes")
+        planes = ring.tile([P, 4 * T], U32, name="planes", tag="planes", align_bytes=64)
 
         def plane(u):
             return planes[:, u * T:(u + 1) * T]
 
-        for q in range(2):
-            nc.vector.tensor_copy(planes[:, q * HALF:(q + 1) * HALF].bitcast(BF16).rearrange("p (t e) -> p t e", e=2), x_head[q][:].rearrange("p e t -> p t e"))
-        nc.scalar.copy(plane(1).bitcast(BF16).rearrange("p (t e) -> p t e", e=2), x_next[:].rearrange("p e t -> p t e"))
-        nc.scalar.copy(planes[:, 2 * T:].bitcast(BF16).rearrange("p (h t e) -> p h t e", h=2, e=2), x_second[:].rearrange("p h e t -> p h t e"))
+        def round_to_bf16(engine, dst, src):
+            if engine == "vector":
+                nc.vector.tensor_copy(dst, src)
+            elif engine == "scalar":
+                nc.scalar.copy(dst, src)
+            else:
+                nc.gpsimd.tensor_scalar(dst, src, 1.0, 0.0, ALU.mult, ALU.add)
 
-        gathered = {}
-        x_codes = {}
-        x_scales = {}
-        w_codes = {}
-        w_scales = {}
+        for q in range(2):
+            round_to_bf16("vector", planes[:, q * HALF:(q + 1) * HALF].bitcast(BF16).rearrange("p (t e) -> p t e", e=2), x_head[q][:].rearrange("p e t -> p t e"))
+        for u in range(1, 4):
+            round_to_bf16("scalar" if u == 1 else "gpsimd", plane(u).bitcast(BF16).rearrange("p (t e) -> p t e", e=2), x_raw[u][:].rearrange("p e t -> p t e"))
+
+        woven = {}
+        w_bf = {}
         y = keep.tile([P, S], F32, name="y")
 
-        def gather(c, g, h):
+        def gather_and_weave(c, g):
             s0, n = CHUNKS[c]
-            if h == 0:
-                gathered[c, g] = ring.tile([P, 2 * n], U32, name="gathered%d_%d" % (c, g), tag="gathered", bufs=5)
-            nc.vector.tensor_copy(gathered[c, g][:, h * n:(h + 1) * n], plane(2 * g + h).indirect(slot_list[:, s0 // 16:(s0 + n) // 16]))
+            gathered = ring.tile([P, 2 * n], U32, name="gathered%d_%d" % (c, g), tag="gathered", bufs=4, align_bytes=64)
+            for h in range(2):
+                nc.vector.tensor_copy(gathered[:, h * n:(h + 1) * n], plane(2 * g + h).indirect(slot_list[:, s0 // 16:(s0 + n) // 16]))
+            woven[c, g] = keep.tile([P, 2 * n], U32, name="woven%d_%d" % (c, g), align_bytes=64)
+            nc.scalar.copy(woven[c, g][:].rearrange("p (s h) -> p s h", h=2), gathered[:].rearrange("p (h s) -> p s h", h=2))
 
-        def quantise(woven, words, name):
-            codes = keep.tile([P, words], U32, name=name + "_codes", align_bytes=64)
-            scales = keep.tile([P, words], U8, name=name + "_scales", align_bytes=64)
-            nc.vector.quantize_mx(out=codes[:].bitcast(FP8X4), scales=scales[:], in_=woven)
+        def round_weights(i):
+            e0, ne = pairs[i]
+            w_bf[i] = ring.tile([P, ne * PASSES * N * 4], BF16, name="w_bf%d" % i, tag="w_bf", bufs=8, align_bytes=64)
+            if i in GPSIMD_PAIRS:
+                for e in range(ne * PASSES):
+                    round_to_bf16("gpsimd", w_bf[i][:, e * 4 * N:(e + 1) * 4 * N].rearrange("p (c i j) -> p c j i", i=4, j=4), w_raw[i][:, e].rearrange("p j (c i) -> p c j i", i=4))
+            else:
+                round_to_bf16("vector" if i in VECTOR_PAIRS else "scalar", w_bf[i][:].rearrange("p (a c i j) -> p a c j i", a=ne * PASSES, i=4, j=4), w_raw[i][:].rearrange("p a j (c i) -> p a c j i", i=4))
+
+        units = [(c, g) for g in range(PASSES) for c in range(len(CHUNKS))]
+        for i, (c, g) in enumerate(units):
+            if i < 7:
+                round_weights(i)
+            gather_and_weave(c, g)
+
+        shared_woven = []
+        for q in range(T // GROUP):
+            tokens = ring.tile([P, PASSES * 2 * GROUP], U32, name="shared_woven%d" % q, tag="gathered", bufs=4, align_bytes=64)
+            nc.vector.tensor_copy(tokens[:].bitcast(I32).rearrange("p (g t h) -> p g t h", g=PASSES, h=2),
+                                  planes[:].bitcast(I32).rearrange("p (g h t) -> p g t h", g=PASSES, h=2)[:, :, q * GROUP:(q + 1) * GROUP, :])
+            shared_woven.append(tokens)
+
+        all_scales = ring.tile([P, PASSES * (S + T + (E + 1) * N)], U8, name="all_scales", tag="planes", align_bytes=64)
+        used = [0]
+
+        def quantise(values, words, name):
+            codes = ring.tile([P, words], U32, name=name + "_codes", tag="codes", bufs=8, align_bytes=64)
+            scales = all_scales[:, used[0]:used[0] + words]
+            used[0] = used[0] + words
+            nc.vector.quantize_mx(out=codes[:].bitcast(FP8X4), scales=scales, in_=values)
             return codes, scales
 
-        def weave_and_quantise(c, g, on_vector):
-            n = CHUNKS[c][1]
-            woven = ring.tile([P, 2 * n], U32, name="woven%d_%d" % (c, g), tag="woven", bufs=3, align_bytes=64)
-            if on_vector:
-                nc.vector.tensor_copy(woven[:].bitcast(I32).rearrange("p (s h) -> p s h", h=2), gathered[c, g][:].bitcast(I32).rearrange("p (h s) -> p s h", h=2))
-            else:
-                nc.scalar.copy(woven[:].rearrange("p (s h) -> p s h", h=2), gathered[c, g][:].rearrange("p (h s) -> p s h", h=2))
-            x_codes[c, g], x_scales[c, g] = quantise(woven[:].bitcast(BF16), n, "x%d_%d" % (c, g))
+        w_codes = {}
+        w_scales = {}
 
-        def weights(i):
+        def quantise_weights(i):
             e0, ne = pairs[i]
-            rounded = ring.tile([P, ne * PASSES * N * 4], BF16, name="w_bf%d" % i, tag="w_bf", bufs=3, align_bytes=64)
-            dst = rounded[:].rearrange("p (a c i j) -> p a c j i", a=ne * PASSES, i=4, j=4)
-            src = w_raw[i][:].rearrange("p a j (c i) -> p a c j i", i=4)
-            if i in VECTOR_PAIRS:
-                nc.vector.tensor_copy(dst, src)
-            else:
-                nc.scalar.copy(dst, src)
-            codes, scales = quantise(rounded[:], ne * PASSES * N, "w%d" % i)
+            codes, scales = quantise(w_bf[i][:], ne * PASSES * N, "w%d" % i)
             for a in range(ne * PASSES):
                 w_codes[e0 + a // PASSES, a % PASSES] = codes[:, a * N:(a + 1) * N]
                 w_scales[e0 + a // PASSES, a % PASSES] = scales[:, a * N:(a + 1) * N]
@@ -119,46 +146,31 @@ def tile_moe_shr_lin_relu2_kernel(tc, xT, w, b, gate, offs, pos1, pos2, pos3, ou
 
         def experts(c):
             s0, n = CHUNKS[c]
+            for i in range(s0 // (2 * C), (s0 + n) // (2 * C)):
+                quantise_weights(i)
+            quantised = [quantise(woven[c, g][:].bitcast(BF16), n, "x%d_%d" % (c, g)) for g in range(PASSES)]
             acc = psum.tile([P, n], F32, name="acc%d" % c, tag="acc", bufs=4)
             positive = ring.tile([P, n], F32, name="positive%d" % c, tag="positive", bufs=2)
             for q in range(n // C):
                 cols = slice(q * C, (q + 1) * C)
-                product(acc[:, cols], s0 // C + q, [x_codes[c, g][:, cols] for g in range(PASSES)], [x_scales[c, g][:, cols] for g in range(PASSES)])
+                product(acc[:, cols], s0 // C + q, [codes[:, cols] for codes, scales in quantised], [scales[:, cols] for codes, scales in quantised])
             for q in range(n // C):
                 cols = slice(q * C, (q + 1) * C)
                 e = s0 // C + q
                 nc.scalar.activation(positive[:, cols], acc[:, cols], ACT.Relu, bias=bias[:, e:e + 1])
             nc.scalar.activation(y[:, s0:s0 + n], positive[:], ACT.Square)
 
-        last = len(CHUNKS) - 1
-        for h in range(2):
-            for c in range(len(CHUNKS)):
-                gather(c, 0, h)
-        early = {1: 0, 3: 1, 4: 2}
         for c in range(len(CHUNKS)):
-            weave_and_quantise(c, 0, False)
-            gather(c, 1, 0)
-            gather(c, 1, 1)
-            if c in early:
-                weights(early[c])
-        weights(3)
-        later = {0: (4,), 1: (5, 6), 2: (7, 8), 3: (9,), 4: ()}
-        for c in range(len(CHUNKS)):
-            weave_and_quantise(c, 1, c == last)
-            if c > 0:
-                experts(c - 1)
-            for i in later[c]:
-                weights(i)
-        experts(last)
+            if 7 + c < len(pairs):
+                round_weights(7 + c)
+            experts(c)
 
         shared = keep.tile([P, T], F32, name="shared")
         shared_acc = [psum.tile([P, 2 * GROUP], F32, name="shared_acc0"), psum.tile([P, GROUP], F32, name="shared_acc1")]
         shared_positive = keep.tile([P, T], F32, name="shared_positive")
+        quantise_weights(len(pairs) - 1)
         for q in range(T // GROUP):
-            woven = ring.tile([P, PASSES * 2 * GROUP], U32, name="woven_shared%d" % q, tag="woven", bufs=3, align_bytes=64)
-            nc.vector.tensor_copy(woven[:].bitcast(I32).rearrange("p (g t h) -> p g t h", g=PASSES, h=2),
-                                  planes[:].bitcast(I32).rearrange("p (g h t) -> p g t h", g=PASSES, h=2)[:, :, q * GROUP:(q + 1) * GROUP, :])
-            codes, scales = quantise(woven[:].bitcast(BF16), PASSES * GROUP, "xs%d" % q)
+            codes, scales = quantise(shared_woven[q][:].bitcast(BF16), PASSES * GROUP, "xs%d" % q)
             product(shared_acc[q // 2][:, (q % 2) * GROUP:(q % 2 + 1) * GROUP], E,
                     [codes[:, g * GROUP:(g + 1) * GROUP] for g in range(PASSES)], [scales[:, g * GROUP:(g + 1) * GROUP] for g in range(PASSES)])
         for acc, t0, n in ((shared_acc[0], 0, 2 * GROUP), (shared_acc[1], 2 * GROUP, GROUP)):
@@ -176,6 +188,6 @@ def tile_moe_shr_lin_relu2_kernel(tc, xT, w, b, gate, offs, pos1, pos2, pos3, ou
             second = ring.tile([P, HALF], F32, name="second%d" % half, tag="second", bufs=2)
             total = ring.tile([P, HALF], F32, name="total%d" % half, tag="total", bufs=2)
             nc.vector.tensor_tensor(first[:], terms[0][:], shared[:, toks], ALU.add)
-            nc.vector.tensor_tensor(second[:], terms[1][:], terms[2][:], ALU.add)
-            nc.vector.tensor_tensor(total[:], first[:], second[:], ALU.add)
+            nc.vector.tensor_tensor(second[:], first[:], terms[1][:], ALU.add)
+            nc.vector.tensor_tensor(total[:], second[:], terms[2][:], ALU.add)
             nc.sync.dma_start(out[:, toks], total[:])

@@ -1,6 +1,7 @@
 from contextlib import ExitStack
 
 import concourse.mybir as mybir
+from concourse.masks import make_identity
 
 K, T, E, C, N = 1024, 768, 18, 128, 128
 TOP = 3
@@ -23,8 +24,17 @@ CHUNK = 512
 CHUNKS = [(s0, min(CHUNK, S - s0)) for s0 in range(0, S, CHUNK)]
 GROUP = 256
 HALF = T // 2
-GPSIMD_PAIRS = (1, 3, 5)
-VECTOR_PAIRS = ()
+FIRST = 512
+GPSIMD_PAIRS = (1, 2, 3)
+VECTOR_PAIRS = (8, 9)
+GPSIMD_PLANES = (2,)
+SHARED_AT = 5
+SHARED_ON_VECTOR = False
+GB = 4
+EARLY = 7
+W_FIRST = 1
+LAST_AT = 4
+WB = 5
 
 
 def tile_moe_shr_lin_relu2_kernel(tc, xT, w, b, gate, offs, pos1, pos2, pos3, out):
@@ -39,7 +49,7 @@ def tile_moe_shr_lin_relu2_kernel(tc, xT, w, b, gate, offs, pos1, pos2, pos3, ou
 
         def load_weights(i):
             e0, ne = pairs[i]
-            raw = ring.tile([P, ne * PASSES, 4, N], F32, name="w_raw%d" % i, tag="w_raw", bufs=5)
+            raw = ring.tile([P, ne * PASSES, 4, N], F32, name="w_raw%d" % i, tag="w_raw", bufs=WB)
             nc.sync.dma_start(raw[:], w[e0:e0 + ne].rearrange("e (g p j) n -> p (e g) j n", g=PASSES, p=P))
             w_raw.append(raw)
 
@@ -51,9 +61,9 @@ def tile_moe_shr_lin_relu2_kernel(tc, xT, w, b, gate, offs, pos1, pos2, pos3, ou
         nc.sync.dma_start(slot_list[:], offs)
         x_raw = {}
         for u in range(1, 4):
-            x_raw[u] = keep.tile([P, 2, T], F32, name="x_raw%d" % u)
+            x_raw[u] = ring.tile([P, 2, T], F32, name="x_raw%d" % u, tag="x_raw", bufs=3)
             nc.sync.dma_start(x_raw[u][:], x_rows[u // 2, :, u % 2, :, :])
-            if u == 1:
+            if u == W_FIRST:
                 load_weights(0)
 
         bias = keep.tile([P, E + 1], F32, name="bias")
@@ -64,10 +74,8 @@ def tile_moe_shr_lin_relu2_kernel(tc, xT, w, b, gate, offs, pos1, pos2, pos3, ou
                 nc.sync.dma_start(bias[:], b)
                 for lst, src in zip(back_lists, (pos1, pos2, pos3)):
                     nc.sync.dma_start(lst[:], src)
-        gates = keep.tile([P, TOP, T], F32, name="gates")
-        nc.sync.dma_start(gates[:], gate.rearrange("r p t -> p r t"))
 
-        planes = ring.tile([P, 4 * T], U32, name="planes", tag="planes", align_bytes=64)
+        planes = keep.tile([P, 4 * T], U32, name="planes")
 
         def plane(u):
             return planes[:, u * T:(u + 1) * T]
@@ -83,7 +91,15 @@ def tile_moe_shr_lin_relu2_kernel(tc, xT, w, b, gate, offs, pos1, pos2, pos3, ou
         for q in range(2):
             round_to_bf16("vector", planes[:, q * HALF:(q + 1) * HALF].bitcast(BF16).rearrange("p (t e) -> p t e", e=2), x_head[q][:].rearrange("p e t -> p t e"))
         for u in range(1, 4):
-            round_to_bf16("scalar" if u == 1 else "gpsimd", plane(u).bitcast(BF16).rearrange("p (t e) -> p t e", e=2), x_raw[u][:].rearrange("p e t -> p t e"))
+            round_to_bf16("gpsimd" if u in GPSIMD_PLANES else "scalar", plane(u).bitcast(BF16).rearrange("p (t e) -> p t e", e=2), x_raw[u][:].rearrange("p e t -> p t e"))
+
+        gates = []
+        for r in range(TOP):
+            gates.append(ring.tile([P, T], F32, name="gates%d" % r, tag="x_raw", bufs=3))
+            nc.sync.dma_start(gates[r][:], gate[r])
+
+        identity = keep.tile([P, P], F32, name="identity")
+        make_identity(nc, identity[:])
 
         woven = {}
         w_bf = {}
@@ -91,7 +107,7 @@ def tile_moe_shr_lin_relu2_kernel(tc, xT, w, b, gate, offs, pos1, pos2, pos3, ou
 
         def gather_and_weave(c, g):
             s0, n = CHUNKS[c]
-            gathered = ring.tile([P, 2 * n], U32, name="gathered%d_%d" % (c, g), tag="gathered", bufs=4, align_bytes=64)
+            gathered = ring.tile([P, 2 * n], U32, name="gathered%d_%d" % (c, g), tag="gathered", bufs=GB, align_bytes=64)
             for h in range(2):
                 nc.vector.tensor_copy(gathered[:, h * n:(h + 1) * n], plane(2 * g + h).indirect(slot_list[:, s0 // 16:(s0 + n) // 16]))
             woven[c, g] = keep.tile([P, 2 * n], U32, name="woven%d_%d" % (c, g), align_bytes=64)
@@ -102,31 +118,36 @@ def tile_moe_shr_lin_relu2_kernel(tc, xT, w, b, gate, offs, pos1, pos2, pos3, ou
             w_bf[i] = ring.tile([P, ne * PASSES * N * 4], BF16, name="w_bf%d" % i, tag="w_bf", bufs=8, align_bytes=64)
             if i in GPSIMD_PAIRS:
                 for e in range(ne * PASSES):
-                    round_to_bf16("gpsimd", w_bf[i][:, e * 4 * N:(e + 1) * 4 * N].rearrange("p (c i j) -> p c j i", i=4, j=4), w_raw[i][:, e].rearrange("p j (c i) -> p c j i", i=4))
+                    round_to_bf16("gpsimd", w_bf[i][:, e * 4 * N:(e + 1) * 4 * N].rearrange("p (n j) -> p n j", j=4), w_raw[i][:, e].rearrange("p j n -> p n j"))
             else:
                 round_to_bf16("vector" if i in VECTOR_PAIRS else "scalar", w_bf[i][:].rearrange("p (a c i j) -> p a c j i", a=ne * PASSES, i=4, j=4), w_raw[i][:].rearrange("p a j (c i) -> p a c j i", i=4))
 
         units = [(c, g) for g in range(PASSES) for c in range(len(CHUNKS))]
-        for i, (c, g) in enumerate(units):
-            if i < 7:
-                round_weights(i)
-            gather_and_weave(c, g)
-
         shared_woven = []
-        for q in range(T // GROUP):
-            tokens = ring.tile([P, PASSES * 2 * GROUP], U32, name="shared_woven%d" % q, tag="gathered", bufs=4, align_bytes=64)
-            nc.vector.tensor_copy(tokens[:].bitcast(I32).rearrange("p (g t h) -> p g t h", g=PASSES, h=2),
-                                  planes[:].bitcast(I32).rearrange("p (g h t) -> p g t h", g=PASSES, h=2)[:, :, q * GROUP:(q + 1) * GROUP, :])
+
+        def weave_shared(q):
+            if SHARED_ON_VECTOR:
+                tokens = ring.tile([P, PASSES * 2 * GROUP], U32, name="shared_woven%d" % q, tag="gathered", bufs=GB, align_bytes=64)
+                nc.vector.tensor_copy(tokens[:].bitcast(I32).rearrange("p (g t h) -> p g t h", g=PASSES, h=2),
+                                      planes[:].bitcast(I32).rearrange("p (g h t) -> p g t h", g=PASSES, h=2)[:, :, q * GROUP:(q + 1) * GROUP, :])
+            else:
+                tokens = keep.tile([P, PASSES * 2 * GROUP], U32, name="shared_woven%d" % q, align_bytes=64)
+                nc.scalar.copy(tokens[:].rearrange("p (g t h) -> p g t h", g=PASSES, h=2),
+                               planes[:].rearrange("p (g h t) -> p g t h", g=PASSES, h=2)[:, :, q * GROUP:(q + 1) * GROUP, :])
             shared_woven.append(tokens)
 
-        all_scales = ring.tile([P, PASSES * (S + T + (E + 1) * N)], U8, name="all_scales", tag="planes", align_bytes=64)
-        used = [0]
+        for i, (c, g) in enumerate(units):
+            if i < EARLY:
+                round_weights(i)
+            gather_and_weave(c, g)
+            if i == SHARED_AT:
+                for q in range(T // GROUP):
+                    weave_shared(q)
 
         def quantise(values, words, name):
             codes = ring.tile([P, words], U32, name=name + "_codes", tag="codes", bufs=8, align_bytes=64)
-            scales = all_scales[:, used[0]:used[0] + words]
-            used[0] = used[0] + words
-            nc.vector.quantize_mx(out=codes[:].bitcast(FP8X4), scales=scales, in_=values)
+            scales = ring.tile([P, words], U8, name=name + "_scales", tag="scales", bufs=8, align_bytes=64)
+            nc.vector.quantize_mx(out=codes[:].bitcast(FP8X4), scales=scales[:], in_=values)
             return codes, scales
 
         w_codes = {}
@@ -161,12 +182,17 @@ def tile_moe_shr_lin_relu2_kernel(tc, xT, w, b, gate, offs, pos1, pos2, pos3, ou
             nc.scalar.activation(y[:, s0:s0 + n], positive[:], ACT.Square)
 
         for c in range(len(CHUNKS)):
-            if 7 + c < len(pairs):
-                round_weights(7 + c)
+            if EARLY + c < len(pairs) - 1:
+                round_weights(EARLY + c)
             experts(c)
+            if c == LAST_AT:
+                round_weights(len(pairs) - 1)
+            for q in range(T // GROUP):
+                if SHARED_AT >= 10 and min(SHARED_AT - 10 + q, 4) == c:
+                    weave_shared(q)
 
         shared = keep.tile([P, T], F32, name="shared")
-        shared_acc = [psum.tile([P, 2 * GROUP], F32, name="shared_acc0"), psum.tile([P, GROUP], F32, name="shared_acc1")]
+        shared_acc = [psum.tile([P, 2 * GROUP], F32, name="shared_acc0", tag="shared_acc0", bufs=1), psum.tile([P, GROUP], F32, name="shared_acc1", tag="shared_acc1", bufs=1)]
         shared_positive = keep.tile([P, T], F32, name="shared_positive")
         quantise_weights(len(pairs) - 1)
         for q in range(T // GROUP):
@@ -177,17 +203,34 @@ def tile_moe_shr_lin_relu2_kernel(tc, xT, w, b, gate, offs, pos1, pos2, pos3, ou
             nc.scalar.activation(shared_positive[:, t0:t0 + n], acc[:], ACT.Relu, bias=bias[:, E:E + 1])
             nc.scalar.activation(shared[:, t0:t0 + n], shared_positive[:, t0:t0 + n], ACT.Square)
 
-        for half in range(2):
-            toks = slice(half * HALF, (half + 1) * HALF)
-            terms = []
-            for r in range(TOP):
-                term = ring.tile([P, HALF], F32, name="term%d_%d" % (half, r), tag="term", bufs=6)
-                nc.vector.tensor_tensor(term[:], y[:].indirect(back_lists[r][:, half * HALF // 16:(half + 1) * HALF // 16]), gates[:, r, toks], ALU.mult)
-                terms.append(term)
-            first = ring.tile([P, HALF], F32, name="first%d" % half, tag="first", bufs=2)
-            second = ring.tile([P, HALF], F32, name="second%d" % half, tag="second", bufs=2)
-            total = ring.tile([P, HALF], F32, name="total%d" % half, tag="total", bufs=2)
-            nc.vector.tensor_tensor(first[:], terms[0][:], shared[:, toks], ALU.add)
-            nc.vector.tensor_tensor(second[:], first[:], terms[1][:], ALU.add)
-            nc.vector.tensor_tensor(total[:], second[:], terms[2][:], ALU.add)
-            nc.sync.dma_start(out[:, toks], total[:])
+        parts = [(0, FIRST), (FIRST, T - FIRST)]
+        terms = {}
+
+        def fetch(r, part):
+            t0, n = parts[part]
+            terms[r, part] = keep.tile([P, n], F32, name="term%d_%d" % (r, part))
+            nc.vector.tensor_tensor(terms[r, part][:], y[:].indirect(back_lists[r][:, t0 // 16:(t0 + n) // 16]), gates[r][:, t0:t0 + n], ALU.mult)
+
+        partial = []
+        for part, (t0, n) in enumerate(parts):
+            fetch(0, part)
+            fetch(1, part)
+            turned = keep.tile([P, n], F32, name="turned%d" % part)
+            back = psum.tile([P, n], F32, name="back%d" % part)
+            for j in range(n // P):
+                cols = slice(j * P, (j + 1) * P)
+                block = psum.tile([P, P], F32, name="block%d_%d" % (part, j), tag="acc" if part == 0 else "shared_acc%d" % j, bufs=4 if part == 0 else 1)
+                addends = (shared[:, t0 + j * P:t0 + (j + 1) * P], terms[0, part][:, cols], terms[1, part][:, cols])
+                for a, addend in enumerate(addends):
+                    nc.tensor.matmul(block[:], addend, identity[:], is_transpose=True, start=(a == 0), stop=(a == len(addends) - 1))
+                nc.scalar.copy(turned[:, cols], block[:])
+            for j in range(n // P):
+                cols = slice(j * P, (j + 1) * P)
+                nc.tensor.transpose(back[:, cols], turned[:, cols], identity[:])
+            partial.append(back)
+        for part in range(2):
+            fetch(2, part)
+        for part, (t0, n) in enumerate(parts):
+            total = keep.tile([P, n], F32, name="total%d" % part)
+            nc.vector.tensor_tensor(total[:], partial[part][:], terms[2, part][:], ALU.add)
+            nc.sync.dma_start(out[:, t0:t0 + n], total[:])

@@ -11,7 +11,6 @@ FLOPS = 2 * K * N * (S + T)
 F32 = mybir.dt.float32
 BF16 = mybir.dt.bfloat16
 U32 = mybir.dt.uint32
-I32 = mybir.dt.int32
 U16 = mybir.dt.uint16
 U8 = mybir.dt.uint8
 FP8X4 = mybir.dt.float8_e4m3fn_x4
@@ -20,21 +19,26 @@ ALU = mybir.AluOpType
 
 P = 128
 PASSES = 2
-CHUNK = 512
+PACK = 4
+PLANES = 2 * PASSES
+PER_COLUMN = 16
+
+CHUNK = 4 * C
 CHUNKS = [(s0, min(CHUNK, S - s0)) for s0 in range(0, S, CHUNK)]
+BATCHES = [(e0, min(2, E + 1 - e0)) for e0 in range(0, E + 1, 2)]
 GROUP = 256
-HALF = T // 2
-FIRST = 512
-GPSIMD_PAIRS = (1, 2, 3)
-VECTOR_PAIRS = (8, 9)
-GPSIMD_PLANES = (2,)
-SHARED_AT = 5
-SHARED_ON_VECTOR = False
-GB = 4
-EARLY = 7
-W_FIRST = 1
-LAST_AT = 4
-WB = 5
+HEAD = T // 2
+PARTS = [(0, 512), (512, T - 512)]
+
+GPSIMD_BATCHES = 3
+VECTOR_BATCHES = 3
+LAG = 4
+
+RAW_BUFS = 5
+ROUNDED_BUFS = 8
+GATHERED_BUFS = 4
+CODE_BUFS = 8
+ACC_BUFS = 4
 
 
 def tile_moe_shr_lin_relu2_kernel(tc, xT, w, b, gate, offs, pos1, pos2, pos3, out):
@@ -44,193 +48,183 @@ def tile_moe_shr_lin_relu2_kernel(tc, xT, w, b, gate, offs, pos1, pos2, pos3, ou
         ring = ctx.enter_context(tc.tile_pool(name="ring", bufs=1))
         psum = ctx.enter_context(tc.psum_pool(name="psum", bufs=1))
 
-        pairs = [(e0, min(2, E + 1 - e0)) for e0 in range(0, E + 1, 2)]
-        w_raw = []
-
-        def load_weights(i):
-            e0, ne = pairs[i]
-            raw = ring.tile([P, ne * PASSES, 4, N], F32, name="w_raw%d" % i, tag="w_raw", bufs=WB)
-            nc.sync.dma_start(raw[:], w[e0:e0 + ne].rearrange("e (g p j) n -> p (e g) j n", g=PASSES, p=P))
-            w_raw.append(raw)
-
-        slot_list = keep.tile([P, S // 16], U16, name="slot_list")
-        x_rows = xT.rearrange("(g p h e) t -> g p h e t", g=PASSES, p=P, h=2)
-        x_head = [keep.tile([P, 2, HALF], F32, name="x_head%d" % q) for q in range(2)]
-        for q in range(2):
-            nc.sync.dma_start(x_head[q][:], x_rows[0, :, 0, :, q * HALF:(q + 1) * HALF])
+        x_rows = xT.rearrange("(g p h f) t -> g p h f t", g=PASSES, p=P, h=2)
+        x_head = [keep.tile([P, 2, HEAD], F32, name="x_head%d" % half) for half in range(2)]
+        for half in range(2):
+            nc.sync.dma_start(x_head[half][:], x_rows[0, :, 0, :, half * HEAD:(half + 1) * HEAD])
+        slot_list = keep.tile([P, S // PER_COLUMN], U16, name="slot_list")
         nc.sync.dma_start(slot_list[:], offs)
         x_raw = {}
-        for u in range(1, 4):
-            x_raw[u] = ring.tile([P, 2, T], F32, name="x_raw%d" % u, tag="x_raw", bufs=3)
+        for u in range(1, PLANES):
+            x_raw[u] = ring.tile([P, 2, T], F32, name="x_raw%d" % u, tag="x_raw", bufs=PLANES - 1)
             nc.sync.dma_start(x_raw[u][:], x_rows[u // 2, :, u % 2, :, :])
-            if u == W_FIRST:
-                load_weights(0)
 
         bias = keep.tile([P, E + 1], F32, name="bias")
-        back_lists = [keep.tile([P, T // 16], U16, name="back_list%d" % r) for r in range(TOP)]
-        for i in range(1, len(pairs)):
-            load_weights(i)
-            if i == 4:
+        back_lists = [keep.tile([P, T // PER_COLUMN], U16, name="back_list%d" % r) for r in range(TOP)]
+        w_raw = []
+        for i, (e0, count) in enumerate(BATCHES):
+            w_raw.append(ring.tile([P, count * PASSES, PACK, N], F32, name="w_raw%d" % i, tag="w_raw", bufs=RAW_BUFS))
+            nc.sync.dma_start(w_raw[i][:], w[e0:e0 + count].rearrange("e (g p j) n -> p (e g) j n", g=PASSES, p=P))
+            if i == RAW_BUFS - 1:
                 nc.sync.dma_start(bias[:], b)
-                for lst, src in zip(back_lists, (pos1, pos2, pos3)):
-                    nc.sync.dma_start(lst[:], src)
+                for back_list, pos in zip(back_lists, (pos1, pos2, pos3)):
+                    nc.sync.dma_start(back_list[:], pos)
 
-        planes = keep.tile([P, 4 * T], U32, name="planes")
+        planes = keep.tile([P, PLANES * T], U32, name="planes")
 
         def plane(u):
             return planes[:, u * T:(u + 1) * T]
 
-        def round_to_bf16(engine, dst, src):
-            if engine == "vector":
-                nc.vector.tensor_copy(dst, src)
-            elif engine == "scalar":
-                nc.scalar.copy(dst, src)
-            else:
-                nc.gpsimd.tensor_scalar(dst, src, 1.0, 0.0, ALU.mult, ALU.add)
+        def as_pairs(words):
+            return words.bitcast(BF16).rearrange("p (t f) -> p t f", f=2)
 
-        for q in range(2):
-            round_to_bf16("vector", planes[:, q * HALF:(q + 1) * HALF].bitcast(BF16).rearrange("p (t e) -> p t e", e=2), x_head[q][:].rearrange("p e t -> p t e"))
-        for u in range(1, 4):
-            round_to_bf16("gpsimd" if u in GPSIMD_PLANES else "scalar", plane(u).bitcast(BF16).rearrange("p (t e) -> p t e", e=2), x_raw[u][:].rearrange("p e t -> p t e"))
+        for half in range(2):
+            nc.vector.tensor_copy(as_pairs(planes[:, half * HEAD:(half + 1) * HEAD]), x_head[half][:].rearrange("p f t -> p t f"))
+        for u in range(1, PLANES):
+            nc.scalar.copy(as_pairs(plane(u)), x_raw[u][:].rearrange("p f t -> p t f"))
 
         gates = []
         for r in range(TOP):
-            gates.append(ring.tile([P, T], F32, name="gates%d" % r, tag="x_raw", bufs=3))
+            gates.append(ring.tile([P, T], F32, name="gates%d" % r, tag="x_raw", bufs=PLANES - 1))
             nc.sync.dma_start(gates[r][:], gate[r])
 
         identity = keep.tile([P, P], F32, name="identity")
         make_identity(nc, identity[:])
 
         woven = {}
-        w_bf = {}
-        y = keep.tile([P, S], F32, name="y")
+        shared_woven = []
+        w_rounded = {}
 
         def gather_and_weave(c, g):
             s0, n = CHUNKS[c]
-            gathered = ring.tile([P, 2 * n], U32, name="gathered%d_%d" % (c, g), tag="gathered", bufs=GB, align_bytes=64)
+            gathered = ring.tile([P, 2 * n], U32, name="gathered%d_%d" % (c, g), tag="gathered", bufs=GATHERED_BUFS, align_bytes=64)
+            offsets = slot_list[:, s0 // PER_COLUMN:(s0 + n) // PER_COLUMN]
             for h in range(2):
-                nc.vector.tensor_copy(gathered[:, h * n:(h + 1) * n], plane(2 * g + h).indirect(slot_list[:, s0 // 16:(s0 + n) // 16]))
+                nc.vector.tensor_copy(gathered[:, h * n:(h + 1) * n], plane(2 * g + h).indirect(offsets))
             woven[c, g] = keep.tile([P, 2 * n], U32, name="woven%d_%d" % (c, g), align_bytes=64)
             nc.scalar.copy(woven[c, g][:].rearrange("p (s h) -> p s h", h=2), gathered[:].rearrange("p (h s) -> p s h", h=2))
 
-        def round_weights(i):
-            e0, ne = pairs[i]
-            w_bf[i] = ring.tile([P, ne * PASSES * N * 4], BF16, name="w_bf%d" % i, tag="w_bf", bufs=8, align_bytes=64)
-            if i in GPSIMD_PAIRS:
-                for e in range(ne * PASSES):
-                    round_to_bf16("gpsimd", w_bf[i][:, e * 4 * N:(e + 1) * 4 * N].rearrange("p (n j) -> p n j", j=4), w_raw[i][:, e].rearrange("p j n -> p n j"))
-            else:
-                round_to_bf16("vector" if i in VECTOR_PAIRS else "scalar", w_bf[i][:].rearrange("p (a c i j) -> p a c j i", a=ne * PASSES, i=4, j=4), w_raw[i][:].rearrange("p a j (c i) -> p a c j i", i=4))
-
-        units = [(c, g) for g in range(PASSES) for c in range(len(CHUNKS))]
-        shared_woven = []
-
         def weave_shared(q):
-            if SHARED_ON_VECTOR:
-                tokens = ring.tile([P, PASSES * 2 * GROUP], U32, name="shared_woven%d" % q, tag="gathered", bufs=GB, align_bytes=64)
-                nc.vector.tensor_copy(tokens[:].bitcast(I32).rearrange("p (g t h) -> p g t h", g=PASSES, h=2),
-                                      planes[:].bitcast(I32).rearrange("p (g h t) -> p g t h", g=PASSES, h=2)[:, :, q * GROUP:(q + 1) * GROUP, :])
-            else:
-                tokens = keep.tile([P, PASSES * 2 * GROUP], U32, name="shared_woven%d" % q, align_bytes=64)
-                nc.scalar.copy(tokens[:].rearrange("p (g t h) -> p g t h", g=PASSES, h=2),
-                               planes[:].rearrange("p (g h t) -> p g t h", g=PASSES, h=2)[:, :, q * GROUP:(q + 1) * GROUP, :])
+            tokens = keep.tile([P, PLANES * GROUP], U32, name="shared_woven%d" % q, align_bytes=64)
+            nc.scalar.copy(
+                tokens[:].rearrange("p (g t h) -> p g t h", g=PASSES, h=2),
+                planes[:].rearrange("p (g h t) -> p g t h", g=PASSES, h=2)[:, :, q * GROUP:(q + 1) * GROUP, :],
+            )
             shared_woven.append(tokens)
 
-        for i, (c, g) in enumerate(units):
-            if i < EARLY:
-                round_weights(i)
+        def round_weights(i):
+            slabs = BATCHES[i][1] * PASSES
+            width = PACK * N
+            w_rounded[i] = ring.tile([P, slabs * width], BF16, name="w_bf%d" % i, tag="w_bf", bufs=ROUNDED_BUFS, align_bytes=64)
+            if i < GPSIMD_BATCHES:
+                for a in range(slabs):
+                    nc.gpsimd.tensor_scalar(
+                        w_rounded[i][:, a * width:(a + 1) * width].rearrange("p (n j) -> p n j", j=PACK),
+                        w_raw[i][:, a].rearrange("p j n -> p n j"), 1.0, 0.0, ALU.mult, ALU.add,
+                    )
+            else:
+                dst = w_rounded[i][:].rearrange("p (a m v j) -> p a m j v", a=slabs, v=4, j=PACK)
+                src = w_raw[i][:].rearrange("p a j (m v) -> p a m j v", v=4)
+                if i >= len(BATCHES) - VECTOR_BATCHES:
+                    nc.vector.tensor_copy(dst, src)
+                else:
+                    nc.scalar.copy(dst, src)
+
+        steps = [(c, g) for g in range(PASSES) for c in range(len(CHUNKS))]
+        for step, (c, g) in enumerate(steps):
+            if step >= LAG:
+                round_weights(step - LAG)
             gather_and_weave(c, g)
-            if i == SHARED_AT:
+            if step == len(CHUNKS) - 1:
                 for q in range(T // GROUP):
                     weave_shared(q)
-
-        def quantise(values, words, name):
-            codes = ring.tile([P, words], U32, name=name + "_codes", tag="codes", bufs=8, align_bytes=64)
-            scales = ring.tile([P, words], U8, name=name + "_scales", tag="scales", bufs=8, align_bytes=64)
-            nc.vector.quantize_mx(out=codes[:].bitcast(FP8X4), scales=scales[:], in_=values)
-            return codes, scales
+        for i in range(len(steps) - LAG, len(BATCHES) - VECTOR_BATCHES):
+            round_weights(i)
 
         w_codes = {}
         w_scales = {}
+        y = keep.tile([P, S], F32, name="y")
+
+        def quantise(values, words, name):
+            codes = ring.tile([P, words], U32, name=name + "_codes", tag="codes", bufs=CODE_BUFS, align_bytes=64)
+            scales = ring.tile([P, words], U8, name=name + "_scales", tag="scales", bufs=CODE_BUFS, align_bytes=64)
+            nc.vector.quantize_mx(out=codes[:].bitcast(FP8X4), scales=scales[:], in_=values)
+            return codes, scales
 
         def quantise_weights(i):
-            e0, ne = pairs[i]
-            codes, scales = quantise(w_bf[i][:], ne * PASSES * N, "w%d" % i)
-            for a in range(ne * PASSES):
+            e0, count = BATCHES[i]
+            codes, scales = quantise(w_rounded[i][:], count * PASSES * N, "w%d" % i)
+            for a in range(count * PASSES):
                 w_codes[e0 + a // PASSES, a % PASSES] = codes[:, a * N:(a + 1) * N]
                 w_scales[e0 + a // PASSES, a % PASSES] = scales[:, a * N:(a + 1) * N]
 
         def product(acc, e, codes, scales):
             for g in range(PASSES):
-                nc.tensor.matmul_mx(out=acc, lhsT=w_codes[e, g].bitcast(FP8X4), lhsT_scale=w_scales[e, g],
-                                    rhs=codes[g].bitcast(FP8X4), rhs_scale=scales[g], start=(g == 0), stop=(g == PASSES - 1))
+                nc.tensor.matmul_mx(
+                    out=acc, lhsT=w_codes[e, g].bitcast(FP8X4), lhsT_scale=w_scales[e, g],
+                    rhs=codes[g].bitcast(FP8X4), rhs_scale=scales[g], start=(g == 0), stop=(g == PASSES - 1),
+                )
 
-        def experts(c):
-            s0, n = CHUNKS[c]
-            for i in range(s0 // (2 * C), (s0 + n) // (2 * C)):
-                quantise_weights(i)
+        for c, (s0, n) in enumerate(CHUNKS):
+            batches = range(s0 // (2 * C), (s0 + n) // (2 * C))
+            for i in batches:
+                if i not in w_rounded:
+                    round_weights(i)
             quantised = [quantise(woven[c, g][:].bitcast(BF16), n, "x%d_%d" % (c, g)) for g in range(PASSES)]
-            acc = psum.tile([P, n], F32, name="acc%d" % c, tag="acc", bufs=4)
+            for i in batches:
+                quantise_weights(i)
+            acc = psum.tile([P, n], F32, name="acc%d" % c, tag="acc", bufs=ACC_BUFS)
+            experts = [(e, slice(e * C - s0, (e + 1) * C - s0)) for e in range(s0 // C, (s0 + n) // C)]
+            for e, cols in experts:
+                product(acc[:, cols], e, [codes[:, cols] for codes, scales in quantised], [scales[:, cols] for codes, scales in quantised])
             positive = ring.tile([P, n], F32, name="positive%d" % c, tag="positive", bufs=2)
-            for q in range(n // C):
-                cols = slice(q * C, (q + 1) * C)
-                product(acc[:, cols], s0 // C + q, [codes[:, cols] for codes, scales in quantised], [scales[:, cols] for codes, scales in quantised])
-            for q in range(n // C):
-                cols = slice(q * C, (q + 1) * C)
-                e = s0 // C + q
+            for e, cols in experts:
                 nc.scalar.activation(positive[:, cols], acc[:, cols], ACT.Relu, bias=bias[:, e:e + 1])
             nc.scalar.activation(y[:, s0:s0 + n], positive[:], ACT.Square)
 
-        for c in range(len(CHUNKS)):
-            if EARLY + c < len(pairs) - 1:
-                round_weights(EARLY + c)
-            experts(c)
-            if c == LAST_AT:
-                round_weights(len(pairs) - 1)
-            for q in range(T // GROUP):
-                if SHARED_AT >= 10 and min(SHARED_AT - 10 + q, 4) == c:
-                    weave_shared(q)
-
+        round_weights(len(BATCHES) - 1)
+        quantise_weights(len(BATCHES) - 1)
         shared = keep.tile([P, T], F32, name="shared")
-        shared_acc = [psum.tile([P, 2 * GROUP], F32, name="shared_acc0", tag="shared_acc0", bufs=1), psum.tile([P, GROUP], F32, name="shared_acc1", tag="shared_acc1", bufs=1)]
         shared_positive = keep.tile([P, T], F32, name="shared_positive")
-        quantise_weights(len(pairs) - 1)
+        shared_acc = [psum.tile([P, n], F32, name="shared_acc%d" % part, tag="shared_acc%d" % part, bufs=1) for part, (t0, n) in enumerate(PARTS)]
+        by_pass = [slice(g * GROUP, (g + 1) * GROUP) for g in range(PASSES)]
         for q in range(T // GROUP):
             codes, scales = quantise(shared_woven[q][:].bitcast(BF16), PASSES * GROUP, "xs%d" % q)
-            product(shared_acc[q // 2][:, (q % 2) * GROUP:(q % 2 + 1) * GROUP], E,
-                    [codes[:, g * GROUP:(g + 1) * GROUP] for g in range(PASSES)], [scales[:, g * GROUP:(g + 1) * GROUP] for g in range(PASSES)])
-        for acc, t0, n in ((shared_acc[0], 0, 2 * GROUP), (shared_acc[1], 2 * GROUP, GROUP)):
+            part, first = divmod(q * GROUP, PARTS[0][1])
+            product(shared_acc[part][:, first:first + GROUP], E, [codes[:, cols] for cols in by_pass], [scales[:, cols] for cols in by_pass])
+        for acc, (t0, n) in zip(shared_acc, PARTS):
             nc.scalar.activation(shared_positive[:, t0:t0 + n], acc[:], ACT.Relu, bias=bias[:, E:E + 1])
             nc.scalar.activation(shared[:, t0:t0 + n], shared_positive[:, t0:t0 + n], ACT.Square)
 
-        parts = [(0, FIRST), (FIRST, T - FIRST)]
         terms = {}
 
         def fetch(r, part):
-            t0, n = parts[part]
+            t0, n = PARTS[part]
             terms[r, part] = keep.tile([P, n], F32, name="term%d_%d" % (r, part))
-            nc.vector.tensor_tensor(terms[r, part][:], y[:].indirect(back_lists[r][:, t0 // 16:(t0 + n) // 16]), gates[r][:, t0:t0 + n], ALU.mult)
+            offsets = back_lists[r][:, t0 // PER_COLUMN:(t0 + n) // PER_COLUMN]
+            nc.vector.tensor_tensor(terms[r, part][:], y[:].indirect(offsets), gates[r][:, t0:t0 + n], ALU.mult)
 
         partial = []
-        for part, (t0, n) in enumerate(parts):
+        for part, (t0, n) in enumerate(PARTS):
             fetch(0, part)
             fetch(1, part)
             turned = keep.tile([P, n], F32, name="turned%d" % part)
             back = psum.tile([P, n], F32, name="back%d" % part)
-            for j in range(n // P):
-                cols = slice(j * P, (j + 1) * P)
-                block = psum.tile([P, P], F32, name="block%d_%d" % (part, j), tag="acc" if part == 0 else "shared_acc%d" % j, bufs=4 if part == 0 else 1)
-                addends = (shared[:, t0 + j * P:t0 + (j + 1) * P], terms[0, part][:, cols], terms[1, part][:, cols])
-                for a, addend in enumerate(addends):
-                    nc.tensor.matmul(block[:], addend, identity[:], is_transpose=True, start=(a == 0), stop=(a == len(addends) - 1))
-                nc.scalar.copy(turned[:, cols], block[:])
-            for j in range(n // P):
-                cols = slice(j * P, (j + 1) * P)
+            squares = [slice(first, first + P) for first in range(0, n, P)]
+            for number, cols in enumerate(squares):
+                tag, bufs = ("acc", ACC_BUFS) if part == 0 else ("shared_acc%d" % number, 1)
+                square = psum.tile([P, P], F32, name="square%d_%d" % (part, number), tag=tag, bufs=bufs)
+                addends = (shared[:, t0:t0 + n][:, cols], terms[0, part][:, cols], terms[1, part][:, cols])
+                for place, addend in enumerate(addends):
+                    nc.tensor.matmul(square[:], addend, identity[:], is_transpose=True, start=(place == 0), stop=(place == len(addends) - 1))
+                nc.scalar.copy(turned[:, cols], square[:])
+            for cols in squares:
                 nc.tensor.transpose(back[:, cols], turned[:, cols], identity[:])
             partial.append(back)
-        for part in range(2):
-            fetch(2, part)
-        for part, (t0, n) in enumerate(parts):
+
+        for part in range(len(PARTS)):
+            fetch(TOP - 1, part)
+        for part, (t0, n) in enumerate(PARTS):
             total = keep.tile([P, n], F32, name="total%d" % part)
-            nc.vector.tensor_tensor(total[:], partial[part][:], terms[2, part][:], ALU.add)
+            nc.vector.tensor_tensor(total[:], partial[part][:], terms[TOP - 1, part][:], ALU.add)
             nc.sync.dma_start(out[:, t0:t0 + n], total[:])

from contextlib import ExitStack

import concourse.mybir as mybir
from concourse.masks import make_identity

K, T, E, C, N = 1024, 768, 18, 128, 128
TOP = 3
S = E * C
FLOPS = 2 * K * N * (S + T)

F32 = mybir.dt.float32
BF16 = mybir.dt.bfloat16
U32 = mybir.dt.uint32
U16 = mybir.dt.uint16
U8 = mybir.dt.uint8
FP8X4 = mybir.dt.float8_e4m3fn_x4
ACT = mybir.ActivationFunctionType
ALU = mybir.AluOpType

P = 128
PASSES = 2
PACK = 4
PLANES = 2 * PASSES
PER_COLUMN = 16

CHUNK = 4 * C
CHUNKS = [(s0, min(CHUNK, S - s0)) for s0 in range(0, S, CHUNK)]
BATCHES = [(e0, min(2, E + 1 - e0)) for e0 in range(0, E + 1, 2)]
GROUP = 256
HEAD = T // 2
PARTS = [(0, 512), (512, T - 512)]

GPSIMD_BATCHES = 3
VECTOR_BATCHES = 3
LAG = 4

RAW_BUFS = 5
ROUNDED_BUFS = 8
GATHERED_BUFS = 4
CODE_BUFS = 8
ACC_BUFS = 4


def tile_moe_shr_lin_relu2_kernel(tc, xT, w, b, gate, offs, pos1, pos2, pos3, out):
    nc = tc.nc
    with ExitStack() as ctx:
        keep = ctx.enter_context(tc.tile_pool(name="keep", bufs=1))
        ring = ctx.enter_context(tc.tile_pool(name="ring", bufs=1))
        psum = ctx.enter_context(tc.psum_pool(name="psum", bufs=1))

        x_rows = xT.rearrange("(g p h f) t -> g p h f t", g=PASSES, p=P, h=2)
        x_head = [keep.tile([P, 2, HEAD], F32, name="x_head%d" % half) for half in range(2)]
        for half in range(2):
            nc.sync.dma_start(x_head[half][:], x_rows[0, :, 0, :, half * HEAD:(half + 1) * HEAD])
        slot_list = keep.tile([P, S // PER_COLUMN], U16, name="slot_list")
        nc.sync.dma_start(slot_list[:], offs)
        x_raw = {}
        for u in range(1, PLANES):
            x_raw[u] = ring.tile([P, 2, T], F32, name="x_raw%d" % u, tag="x_raw", bufs=PLANES - 1)
            nc.sync.dma_start(x_raw[u][:], x_rows[u // 2, :, u % 2, :, :])

        bias = keep.tile([P, E + 1], F32, name="bias")
        back_lists = [keep.tile([P, T // PER_COLUMN], U16, name="back_list%d" % r) for r in range(TOP)]
        w_raw = []
        for i, (e0, count) in enumerate(BATCHES):
            w_raw.append(ring.tile([P, count * PASSES, PACK, N], F32, name="w_raw%d" % i, tag="w_raw", bufs=RAW_BUFS))
            nc.sync.dma_start(w_raw[i][:], w[e0:e0 + count].rearrange("e (g p j) n -> p (e g) j n", g=PASSES, p=P))
            if i == RAW_BUFS - 1:
                nc.sync.dma_start(bias[:], b)
                for back_list, pos in zip(back_lists, (pos1, pos2, pos3)):
                    nc.sync.dma_start(back_list[:], pos)

        planes = keep.tile([P, PLANES * T], U32, name="planes")

        def plane(u):
            return planes[:, u * T:(u + 1) * T]

        def as_pairs(words):
            return words.bitcast(BF16).rearrange("p (t f) -> p t f", f=2)

        for half in range(2):
            nc.vector.tensor_copy(as_pairs(planes[:, half * HEAD:(half + 1) * HEAD]), x_head[half][:].rearrange("p f t -> p t f"))
        for u in range(1, PLANES):
            nc.scalar.copy(as_pairs(plane(u)), x_raw[u][:].rearrange("p f t -> p t f"))

        gates = []
        for r in range(TOP):
            gates.append(ring.tile([P, T], F32, name="gates%d" % r, tag="x_raw", bufs=PLANES - 1))
            nc.sync.dma_start(gates[r][:], gate[r])

        identity = keep.tile([P, P], F32, name="identity")
        make_identity(nc, identity[:])

        woven = {}
        shared_woven = []
        w_rounded = {}

        def gather_and_weave(c, g):
            s0, n = CHUNKS[c]
            gathered = ring.tile([P, 2 * n], U32, name="gathered%d_%d" % (c, g), tag="gathered", bufs=GATHERED_BUFS, align_bytes=64)
            offsets = slot_list[:, s0 // PER_COLUMN:(s0 + n) // PER_COLUMN]
            for h in range(2):
                nc.vector.tensor_copy(gathered[:, h * n:(h + 1) * n], plane(2 * g + h).indirect(offsets))
            woven[c, g] = keep.tile([P, 2 * n], U32, name="woven%d_%d" % (c, g), align_bytes=64)
            nc.scalar.copy(woven[c, g][:].rearrange("p (s h) -> p s h", h=2), gathered[:].rearrange("p (h s) -> p s h", h=2))

        def weave_shared(q):
            tokens = keep.tile([P, PLANES * GROUP], U32, name="shared_woven%d" % q, align_bytes=64)
            nc.scalar.copy(
                tokens[:].rearrange("p (g t h) -> p g t h", g=PASSES, h=2),
                planes[:].rearrange("p (g h t) -> p g t h", g=PASSES, h=2)[:, :, q * GROUP:(q + 1) * GROUP, :],
            )
            shared_woven.append(tokens)

        def round_weights(i):
            slabs = BATCHES[i][1] * PASSES
            width = PACK * N
            w_rounded[i] = ring.tile([P, slabs * width], BF16, name="w_bf%d" % i, tag="w_bf", bufs=ROUNDED_BUFS, align_bytes=64)
            if i < GPSIMD_BATCHES:
                for a in range(slabs):
                    nc.gpsimd.tensor_scalar(
                        w_rounded[i][:, a * width:(a + 1) * width].rearrange("p (n j) -> p n j", j=PACK),
                        w_raw[i][:, a].rearrange("p j n -> p n j"), 1.0, 0.0, ALU.mult, ALU.add,
                    )
            else:
                dst = w_rounded[i][:].rearrange("p (a m v j) -> p a m j v", a=slabs, v=4, j=PACK)
                src = w_raw[i][:].rearrange("p a j (m v) -> p a m j v", v=4)
                if i >= len(BATCHES) - VECTOR_BATCHES:
                    nc.vector.tensor_copy(dst, src)
                else:
                    nc.scalar.copy(dst, src)

        steps = [(c, g) for g in range(PASSES) for c in range(len(CHUNKS))]
        for step, (c, g) in enumerate(steps):
            if step >= LAG:
                round_weights(step - LAG)
            gather_and_weave(c, g)
            if step == len(CHUNKS) - 1:
                for q in range(T // GROUP):
                    weave_shared(q)
        for i in range(len(steps) - LAG, len(BATCHES) - VECTOR_BATCHES):
            round_weights(i)

        w_codes = {}
        w_scales = {}
        y = keep.tile([P, S], F32, name="y")

        def quantise(values, words, name):
            codes = ring.tile([P, words], U32, name=name + "_codes", tag="codes", bufs=CODE_BUFS, align_bytes=64)
            scales = ring.tile([P, words], U8, name=name + "_scales", tag="scales", bufs=CODE_BUFS, align_bytes=64)
            nc.vector.quantize_mx(out=codes[:].bitcast(FP8X4), scales=scales[:], in_=values)
            return codes, scales

        def quantise_weights(i):
            e0, count = BATCHES[i]
            codes, scales = quantise(w_rounded[i][:], count * PASSES * N, "w%d" % i)
            for a in range(count * PASSES):
                w_codes[e0 + a // PASSES, a % PASSES] = codes[:, a * N:(a + 1) * N]
                w_scales[e0 + a // PASSES, a % PASSES] = scales[:, a * N:(a + 1) * N]

        def product(acc, e, codes, scales):
            for g in range(PASSES):
                nc.tensor.matmul_mx(
                    out=acc, lhsT=w_codes[e, g].bitcast(FP8X4), lhsT_scale=w_scales[e, g],
                    rhs=codes[g].bitcast(FP8X4), rhs_scale=scales[g], start=(g == 0), stop=(g == PASSES - 1),
                )

        for c, (s0, n) in enumerate(CHUNKS):
            batches = range(s0 // (2 * C), (s0 + n) // (2 * C))
            for i in batches:
                if i not in w_rounded:
                    round_weights(i)
            quantised = [quantise(woven[c, g][:].bitcast(BF16), n, "x%d_%d" % (c, g)) for g in range(PASSES)]
            for i in batches:
                quantise_weights(i)
            acc = psum.tile([P, n], F32, name="acc%d" % c, tag="acc", bufs=ACC_BUFS)
            experts = [(e, slice(e * C - s0, (e + 1) * C - s0)) for e in range(s0 // C, (s0 + n) // C)]
            for e, cols in experts:
                product(acc[:, cols], e, [codes[:, cols] for codes, scales in quantised], [scales[:, cols] for codes, scales in quantised])
            positive = ring.tile([P, n], F32, name="positive%d" % c, tag="positive", bufs=2)
            for e, cols in experts:
                nc.scalar.activation(positive[:, cols], acc[:, cols], ACT.Relu, bias=bias[:, e:e + 1])
            nc.scalar.activation(y[:, s0:s0 + n], positive[:], ACT.Square)

        round_weights(len(BATCHES) - 1)
        quantise_weights(len(BATCHES) - 1)
        shared = keep.tile([P, T], F32, name="shared")
        shared_positive = keep.tile([P, T], F32, name="shared_positive")
        shared_acc = [psum.tile([P, n], F32, name="shared_acc%d" % part, tag="shared_acc%d" % part, bufs=1) for part, (t0, n) in enumerate(PARTS)]
        by_pass = [slice(g * GROUP, (g + 1) * GROUP) for g in range(PASSES)]
        for q in range(T // GROUP):
            codes, scales = quantise(shared_woven[q][:].bitcast(BF16), PASSES * GROUP, "xs%d" % q)
            part, first = divmod(q * GROUP, PARTS[0][1])
            product(shared_acc[part][:, first:first + GROUP], E, [codes[:, cols] for cols in by_pass], [scales[:, cols] for cols in by_pass])
        for acc, (t0, n) in zip(shared_acc, PARTS):
            nc.scalar.activation(shared_positive[:, t0:t0 + n], acc[:], ACT.Relu, bias=bias[:, E:E + 1])
            nc.scalar.activation(shared[:, t0:t0 + n], shared_positive[:, t0:t0 + n], ACT.Square)

        terms = {}

        def fetch(r, part):
            t0, n = PARTS[part]
            terms[r, part] = keep.tile([P, n], F32, name="term%d_%d" % (r, part))
            offsets = back_lists[r][:, t0 // PER_COLUMN:(t0 + n) // PER_COLUMN]
            nc.vector.tensor_tensor(terms[r, part][:], y[:].indirect(offsets), gates[r][:, t0:t0 + n], ALU.mult)

        partial = []
        for part, (t0, n) in enumerate(PARTS):
            fetch(0, part)
            fetch(1, part)
            turned = keep.tile([P, n], F32, name="turned%d" % part)
            back = psum.tile([P, n], F32, name="back%d" % part)
            squares = [slice(first, first + P) for first in range(0, n, P)]
            for number, cols in enumerate(squares):
                tag, bufs = ("acc", ACC_BUFS) if part == 0 else ("shared_acc%d" % number, 1)
                square = psum.tile([P, P], F32, name="square%d_%d" % (part, number), tag=tag, bufs=bufs)
                addends = (shared[:, t0:t0 + n][:, cols], terms[0, part][:, cols], terms[1, part][:, cols])
                for place, addend in enumerate(addends):
                    nc.tensor.matmul(square[:], addend, identity[:], is_transpose=True, start=(place == 0), stop=(place == len(addends) - 1))
                nc.scalar.copy(turned[:, cols], square[:])
            for cols in squares:
                nc.tensor.transpose(back[:, cols], turned[:, cols], identity[:])
            partial.append(back)

        for part in range(len(PARTS)):
            fetch(TOP - 1, part)
        for part, (t0, n) in enumerate(PARTS):
            total = keep.tile([P, n], F32, name="total%d" % part)
            nc.vector.tensor_tensor(total[:], partial[part][:], terms[TOP - 1, part][:], ALU.add)
            nc.sync.dma_start(out[:, t0:t0 + n], total[:])
